import numpy as np
import ml_dtypes


def mxq(x, axis, fmt="e4m3"):
    dtype, down = {"e4m3": (ml_dtypes.float8_e4m3fn, 7), "e5m2": (ml_dtypes.float8_e5m2, 14)}[fmt]
    v = np.moveaxis(np.asarray(x, np.float32).astype(ml_dtypes.bfloat16).astype(np.float64), axis, -1)
    blocks = v.reshape(v.shape[:-1] + (-1, 32))
    amax = np.abs(blocks).max(-1, keepdims=True)
    byte = np.maximum(np.where(amax > 0, np.frexp(amax)[1] - 1 + 127, 0) - down, 1)
    scale = np.exp2(byte - 127.0)
    codes = (blocks / scale).astype(np.float32).astype(dtype).astype(np.float64)
    return np.moveaxis((codes * scale).reshape(v.shape), -1, axis)


WIDE = False


def mx_kscale(k):
    if not WIDE:
        return np.ones(k)
    levels = np.array([30, -30])
    if k % 512:
        return np.exp2(np.random.permutation(np.resize(levels, k // 32))).repeat(32)
    a = np.empty((k // 512, 16))
    for p in range(k // 512):
        a[p, :8] = np.random.permutation(np.resize(levels, 8))
        for g in range(8):
            far = levels[np.abs(levels - a[p, g]) >= 10]
            a[p, g + 8] = far[np.random.randint(len(far))]
    return np.exp2(a.ravel()).repeat(32)


def f64(x):
    return np.asarray(x).astype(np.float64)


def striped(idx):
    return np.tile(np.asarray(idx).reshape(-1, 16).T, (8, 1)).astype(np.uint16)


def unstriped(offs):
    return offs[:16].T.reshape(-1).astype(np.int64)


def striped8(idx):
    return np.asarray(idx).reshape(8, -1, 16).transpose(0, 2, 1).reshape(128, -1).astype(np.uint16)


def unstriped8(offs):
    return offs.reshape(8, 16, -1).transpose(0, 2, 1).reshape(8, -1).astype(np.int64)


def pick8(x, idx, run):
    r = np.arange(len(x))
    return x[r[:, None], idx[r % (8 * run) // run]]


E2M1 = np.array([0.0, 0.5, 1.0, 1.5, 2.0, 3.0, 4.0, 6.0, -0.0, -0.5, -1.0, -1.5, -2.0, -3.0, -4.0, -6.0])


def pack_weight(w, fmt):
    k, n = w.shape
    w = f64(np.asarray(w, np.float32).astype(ml_dtypes.bfloat16)).reshape(k // 32, 32, n)
    amax = np.abs(w).max(1)
    if fmt in ("e4m3", "e5m2"):
        byte = np.frexp(amax)[1] - 1 + 127 - (7 if fmt == "e4m3" else 14)
    else:
        mant, ex = np.frexp(amax / 6.0)
        byte = np.where(mant > 0.5, ex, ex - 1) + 127
    byte = np.clip(np.where(amax > 0, byte, 1), 1, 254)
    scaled = (w * np.exp2(127.0 - byte)[:, None, :]).reshape(k, n).astype(np.float32)
    by_word = np.ascontiguousarray(scaled.reshape(k // 512, 128, 4, n).transpose(0, 1, 3, 2))
    if fmt in ("e4m3", "e5m2"):
        words = by_word.astype(ml_dtypes.float8_e4m3fn if fmt == "e4m3" else ml_dtypes.float8_e5m2).view(np.uint8)
    else:
        c = by_word.astype(ml_dtypes.float4_e2m1fn).view(np.uint8) & 0xF
        words = (c[..., 0::2] | (c[..., 1::2] << 4)).reshape(k // 512, 128, 2 * n)
    return np.ascontiguousarray(words), np.ascontiguousarray(byte.astype(np.uint8).reshape(k // 512, 16, n))


def unpack_weight(words, scales, fmt):
    g, _, n = scales.shape
    words = np.ascontiguousarray(words).reshape(g, 128, n, -1)
    if fmt in ("e4m3", "e5m2"):
        vals = words.view(ml_dtypes.float8_e4m3fn if fmt == "e4m3" else ml_dtypes.float8_e5m2).astype(np.float64)
    else:
        nib = np.empty((g, 128, n, 4), np.uint8)
        nib[..., 0::2] = words & 0xF
        nib[..., 1::2] = words >> 4
        vals = E2M1[nib]
    vals = vals * np.repeat(np.exp2(scales.astype(np.float64) - 127.0), 8, axis=1)[..., None]
    return vals.transpose(0, 1, 3, 2).reshape(g * 512, n)


K, T, J, R, F, Z, C, O, N = 512, 1024, 256, 512, 512, 1024, 512, 128, 256


def setup_inputs():
    n = np.random.standard_normal
    idx = np.random.permutation(T)[:J]
    idx2 = np.random.permutation(Z)[:J]
    idx3 = np.stack([np.random.permutation(C)[:J] for _ in range(8)])
    idx4 = np.stack([np.random.permutation(C)[:O] for _ in range(8)])
    idx5 = np.stack([np.random.permutation(C)[:O] for _ in range(8)])
    fk = mx_kscale(K)
    ff = mx_kscale(F)
    fr = mx_kscale(R)
    xtp = pack_weight(n((K, T)) / fk[:, None], "e5m2")
    xop = pack_weight(n((F, Z)) / ff[:, None], "e4m3")
    wp = pack_weight(n((K, R)) * 1 / np.sqrt(K) * fk[:, None] * fr, "e2m1")
    w0p = pack_weight(n((F, R)) * 1 / np.sqrt(F) * ff[:, None] * fr, "e2m1")
    wbp = pack_weight(n((R, N)) * 1 / np.sqrt(R) / fr[:, None], "e2m1")
    return {
        "xt_words": xtp[0],
        "xt_scales": xtp[1],
        "xo_words": xop[0],
        "xo_scales": xop[1],
        "w_words": wp[0],
        "w_scales": wp[1],
        "w0_words": w0p[0],
        "w0_scales": w0p[1],
        "sa": (np.random.uniform(0.5, 1.6, (R, 1))).astype(np.float32),
        "sb": (np.random.uniform(0.5, 1.6, (R, 1))).astype(np.float32),
        "wb_words": wbp[0],
        "wb_scales": wbp[1],
        "offs": striped(idx),
        "offs2": striped(idx2),
        "offs3": striped8(idx3),
        "offs4": striped8(idx4),
        "offs5": striped8(idx5),
    }


def reference(xt_words, xt_scales, xo_words, xo_scales, w_words, w_scales, w0_words, w0_scales, sa, sb, wb_words, wb_scales, offs, offs2, offs3, offs4, offs5):
    idx = unstriped(offs)
    idx2 = unstriped(offs2)
    idx3 = unstriped8(offs3)
    idx4 = unstriped8(offs4)
    idx5 = unstriped8(offs5)
    xtu = unpack_weight(xt_words, xt_scales, "e5m2")
    xou = unpack_weight(xo_words, xo_scales, "e4m3")
    wu = unpack_weight(w_words, w_scales, "e2m1")
    w0u = unpack_weight(w0_words, w0_scales, "e2m1")
    wbu = unpack_weight(wb_words, wb_scales, "e2m1")
    xtidxg = xtu[:, idx]
    xoidx2g = xou[:, idx2]
    a = wu.T @ xtidxg + w0u.T @ xoidx2g
    pw = np.zeros((R, C))
    pw[np.arange(R)[:, None], idx3[np.arange(R) % 512 // 64]] = a
    hid = np.maximum(pick8(pw, idx4, 64) * f64(sa), pick8(pw, idx5, 64) * f64(sb))
    hidq = mxq(hid, 0, "e4m3")
    y = wbu.T @ hidq
    return y

@@ -1,0 +1,189 @@
+from contextlib import ExitStack
+
+import concourse.mybir as mybir
+
+FLOPS = 301989888
+
+F32 = mybir.dt.float32
+BF16 = mybir.dt.bfloat16
+I32 = mybir.dt.int32
+U32 = mybir.dt.uint32
+U16 = mybir.dt.uint16
+U8 = mybir.dt.uint8
+E4M3 = mybir.dt.float8_e4m3fn_x4
+E5M2 = mybir.dt.float8_e5m2_x4
+E2M1 = mybir.dt.float4_e2m1fn_x4
+COPY = mybir.ActivationFunctionType.Copy
+MAX = mybir.AluOpType.max
+
+P = 128
+T = 1024
+J = 256
+R = 512
+C = 512
+O = 128
+N = 256
+PACK = 4
+HALF = J // 2
+
+
+def tile_list_ownreads_bank_one_plain_kernel(
+    tc, xt_words, xt_scales, xo_words, xo_scales, w_words, w_scales, w0_words, w0_scales,
+    sa, sb, wb_words, wb_scales, offs, offs2, offs3, offs4, offs5, out,
+):
+    nc = tc.nc
+    with ExitStack() as ctx:
+        keep = ctx.enter_context(tc.tile_pool(name="keep", bufs=1))
+        psum = ctx.enter_context(tc.psum_pool(name="psum", bufs=1))
+
+        def sb_tile(shape, dtype, name, tag=None):
+            return keep.tile(shape, dtype, name=name, tag=tag or name, align_bytes=64)
+
+        xt_stage = sb_tile([4, 4, T // 4], I32, "xt_stage")
+        xo_stage = sb_tile([64, 2, T // 4], I32, "xo_stage")
+        xt_plane = sb_tile([P, T], U8, "xt_plane")
+        xo_plane = sb_tile([P, T], U8, "xo_plane")
+        xt_tab = sb_tile([P, T], U32, "xt_tab")
+        xo_tab = sb_tile([P, T], U32, "xo_tab")
+        w_raw = [sb_tile([P, R], U16, "w_raw%d" % i) for i in range(2)]
+        ws_raw = sb_tile([P, 4, 2, R], U8, "ws_raw")
+        w_dealt = [sb_tile([P, PACK, P], U16, "w_dealt%d" % i) for i in range(2)]
+        ws_dealt = sb_tile([P, PACK, 2, P], U8, "ws_dealt")
+        lists = [sb_tile([P, 16], U16, "list%d" % i) for i in range(3)] + [sb_tile([P, 8], U16, "list%d" % i) for i in (3, 4)]
+        sa_t = sb_tile([P, PACK], F32, "sa_t")
+        sb_t = sb_tile([P, PACK], F32, "sb_t")
+        wb_t = sb_tile([P, 2 * N], U8, "wb_t")
+        wbs_t = sb_tile([P, N], U8, "wbs_t")
+        board = [sb_tile([P, C], F32, "board%d" % t) for t in range(PACK)]
+
+        nc.vector.memset(xo_stage[:], 0)
+        nc.vector.memset(ws_raw[:, 0].bitcast(I32), 0)
+        nc.vector.memset(xt_plane[:].bitcast(I32), 0)
+        nc.vector.memset(board[0][:], 0.0)
+        nc.vector.memset(board[1][:], 0.0)
+        nc.gpsimd.memset(wbs_t[:].bitcast(I32), 0)
+        nc.gpsimd.memset(board[2][:], 0.0)
+        nc.gpsimd.memset(board[3][:], 0.0)
+
+        def words(ap):
+            return ap[0].rearrange("p n t -> p (n t)").bitcast(I32)
+
+        def by_pairs(ap, b):
+            return ap[0].bitcast(I32).rearrange("(a b r) n -> b r a n", a=2, b=2)[b]
+
+        nc.scalar.dma_start(xt_stage[:], xt_scales[0].bitcast(I32).rearrange("(q r) n -> r q n", r=4))
+        nc.sync.dma_start(lists[0][:], offs)
+        nc.sync.dma_start(w_raw[0][:].bitcast(I32), w_words[0].bitcast(I32))
+        nc.sync.dma_start(w_raw[1][:].bitcast(I32), w0_words[0].bitcast(I32))
+        for b in range(2):
+            nc.scalar.dma_start(xo_stage[32 * b : 32 * b + 4], by_pairs(xo_scales, b))
+        nc.sync.dma_start(xt_tab[:].bitcast(I32), words(xt_words))
+        nc.sync.dma_start(lists[1][:], offs2)
+        for i, src in enumerate((w_scales, w0_scales)):
+            nc.sync.dma_start(ws_raw[0:4, :, i, :].bitcast(I32), src[0].bitcast(I32).rearrange("(q r) n -> r q n", r=4))
+        nc.sync.dma_start(xo_tab[:].bitcast(I32), words(xo_words))
+        nc.sync.dma_start(lists[2][:], offs3)
+        nc.sync.dma_start(lists[3][:], offs4)
+        nc.sync.dma_start(sa_t[:], sa.rearrange("(p t) o -> p (t o)", t=PACK))
+        nc.sync.dma_start(lists[4][:], offs5)
+        nc.sync.dma_start(sb_t[:], sb.rearrange("(p t) o -> p (t o)", t=PACK))
+        nc.sync.dma_start(wb_t[:].bitcast(I32), wb_words[0].bitcast(I32))
+        for q in range(4):
+            nc.sync.dma_start(wbs_t[32 * q : 32 * q + 4].bitcast(I32), wb_scales[0, 4 * q : 4 * q + 4].bitcast(I32))
+
+        for q in range(4):
+            nc.vector.tensor_copy(xt_plane[32 * q : 32 * q + 4].bitcast(I32), xt_stage[:, q, :])
+
+        tabs = ((xt_tab, xt_plane, lists[0], E5M2), (xo_tab, xo_plane, lists[1], E4M3))
+
+        def gather_scales(i, half):
+            got = sb_tile([P, HALF], U8, "got_s%d_%d" % (i, half), tag="got_s%d" % i)
+            nc.vector.tensor_copy(got[:], tabs[i][1][:].indirect(tabs[i][2][:, 8 * half : 8 * half + 8]))
+            return got
+
+        def gather_words(i, half):
+            got = sb_tile([P, HALF], U32, "got_w%d_%d" % (i, half), tag="got_w%d" % i)
+            nc.vector.tensor_copy(got[:], tabs[i][0][:].indirect(tabs[i][2][:, 8 * half : 8 * half + 8]))
+            return got
+
+        for i in range(2):
+            nc.scalar.copy(w_dealt[i][:], w_raw[i][:].rearrange("p (m t) -> p t m", t=PACK))
+
+        def deal(t0, t1):
+            nc.vector.tensor_copy(ws_dealt[:, t0:t1], ws_raw[:, 0].rearrange("p i (m t) -> p t i m", t=PACK)[:, t0:t1])
+
+        got_s = [gather_scales(0, 0), None]
+        for a in range(2):
+            nc.vector.tensor_copy(xo_plane[64 * a : 64 * a + 64].bitcast(I32), xo_stage[:, a, :])
+        got_s[1] = gather_scales(1, 0)
+        got_w = [gather_words(0, 0), None]
+        for q in range(1, 4):
+            nc.vector.tensor_copy(ws_raw[32 * q : 32 * q + 4, 0].bitcast(I32), ws_raw[0:4, q].bitcast(I32))
+        deal(0, 1)
+        got_w[1] = gather_words(1, 0)
+
+        def product(acc, t):
+            for i in range(2):
+                nc.tensor.matmul_mx(
+                    out=acc, lhsT=w_dealt[i][:, t, :].bitcast(E2M1), lhsT_scale=ws_dealt[:, t, i, :],
+                    rhs=got_w[i][:].bitcast(tabs[i][3]), rhs_scale=got_s[i][:], start=(i == 0), stop=(i == 1),
+                )
+
+        def place(t, half, src):
+            nc.scalar.activation(board[t][:].indirect(lists[2][:, 8 * half : 8 * half + 8]), src, COPY)
+
+        for t in range(PACK):
+            acc = psum.tile([P, HALF], F32, name="accA%d" % t)
+            product(acc[:], t)
+            a_sb = sb_tile([P, HALF], F32, "aA%d" % t)
+            if t == 0:
+                nc.scalar.activation(a_sb[:], acc[:], COPY)
+            else:
+                nc.vector.tensor_copy(a_sb[:], acc[:])
+            place(t, 0, a_sb[:])
+            if t == 0:
+                deal(1, PACK)
+
+        got_s = [gather_scales(0, 1), gather_scales(1, 1)]
+        got_w = [gather_words(0, 1), gather_words(1, 1)]
+        a_second = []
+        for u in range(2):
+            acc = psum.tile([P, 2, HALF], F32, name="accB%d" % u)
+            for v in range(2):
+                product(acc[:, v, :], 2 * u + v)
+            a_sb = sb_tile([P, 2, HALF], F32, "aB%d" % u)
+            nc.vector.tensor_copy(a_sb[:], acc[:])
+            a_second.extend([a_sb[:, 0, :], a_sb[:, 1, :]])
+
+        hid = sb_tile([P, O, PACK], BF16, "hid")
+
+        def fetch(t):
+            ga = sb_tile([P, O], F32, "ga%d" % t)
+            gb = sb_tile([P, O], F32, "gb%d" % t)
+            nc.scalar.activation(ga[:], board[t][:].indirect(lists[3][:]), COPY, scale=sa_t[:, t : t + 1])
+            nc.scalar.activation(gb[:], board[t][:].indirect(lists[4][:]), COPY, scale=sb_t[:, t : t + 1])
+            nc.vector.tensor_tensor(hid[:, :, t], ga[:], gb[:], MAX)
+
+        place(0, 1, a_second[0])
+        for t in range(1, PACK):
+            place(t, 1, a_second[t])
+            fetch(t - 1)
+        fetch(PACK - 1)
+
+        codes = sb_tile([P, O], U32, "codes")
+        plane = sb_tile([P, O], U8, "plane")
+        nc.vector.quantize_mx(codes[:].bitcast(E4M3), plane[:], hid[:].rearrange("p o t -> p (o t)"))
+
+        for h in range(2):
+            acc = psum.tile([P, O], F32, name="accY%d" % h)
+            nc.tensor.matmul_mx(
+                out=acc[:], lhsT=wb_t[:, 2 * P * h : 2 * P * (h + 1)].bitcast(E2M1), lhsT_scale=wbs_t[:, P * h : P * (h + 1)],
+                rhs=codes[:].bitcast(E4M3), rhs_scale=plane[:], start=True, stop=True,
+            )
+            y = sb_tile([P, O], F32, "y%d" % h)
+            if h == 0:
+                nc.vector.tensor_copy(y[:], acc[:])
+                nc.sync.dma_start(out[0:P, :], y[:])
+            else:
+                nc.scalar.copy(y[:], acc[:])
+                nc.scalar.dma_start(out[P : 2 * P, :], y[:])

@@ -40,7 +40,7 @@ def tile_list_ownreads_bank_one_plain_kernel(
             return keep.tile(shape, dtype, name=name, tag=tag or name, align_bytes=64)
 
         xt_stage = sb_tile([4, 4, T // 4], I32, "xt_stage")
-        xo_stage = sb_tile([64, 2, T // 4], I32, "xo_stage")
+        xo_stage = sb_tile([P, 2, T // 4], I32, "xo_stage")
         xt_plane = sb_tile([P, T], U8, "xt_plane")
         xo_plane = sb_tile([P, T], U8, "xo_plane")
         xt_tab = sb_tile([P, T], U32, "xt_tab")
@@ -54,16 +54,14 @@ def tile_list_ownreads_bank_one_plain_kernel(
         sb_t = sb_tile([P, PACK], F32, "sb_t")
         wb_t = sb_tile([P, 2 * N], U8, "wb_t")
         wbs_t = sb_tile([P, N], U8, "wbs_t")
-        board = [sb_tile([P, C], F32, "board%d" % t) for t in range(PACK)]
+        board = [sb_tile([P, C], F32, "board%d" % t) for t in range(2)]
 
-        nc.vector.memset(xo_stage[:], 0)
         nc.vector.memset(ws_raw[:, 0].bitcast(I32), 0)
+        nc.vector.memset(xo_stage[64:128], 0)
         nc.vector.memset(xt_plane[:].bitcast(I32), 0)
-        nc.vector.memset(board[0][:], 0.0)
-        nc.vector.memset(board[1][:], 0.0)
+        for t in range(2):
+            nc.vector.memset(board[t][:], 0.0)
         nc.gpsimd.memset(wbs_t[:].bitcast(I32), 0)
-        nc.gpsimd.memset(board[2][:], 0.0)
-        nc.gpsimd.memset(board[3][:], 0.0)
 
         def words(ap):
             return ap[0].rearrange("p n t -> p (n t)").bitcast(I32)
@@ -71,17 +69,17 @@ def tile_list_ownreads_bank_one_plain_kernel(
         def by_pairs(ap, b):
             return ap[0].bitcast(I32).rearrange("(a b r) n -> b r a n", a=2, b=2)[b]
 
-        nc.scalar.dma_start(xt_stage[:], xt_scales[0].bitcast(I32).rearrange("(q r) n -> r q n", r=4))
+        nc.sync.dma_start(xt_stage[:], xt_scales[0].bitcast(I32).rearrange("(q r) n -> r q n", r=4))
         nc.sync.dma_start(lists[0][:], offs)
-        nc.sync.dma_start(w_raw[0][:].bitcast(I32), w_words[0].bitcast(I32))
-        nc.sync.dma_start(w_raw[1][:].bitcast(I32), w0_words[0].bitcast(I32))
-        for b in range(2):
-            nc.scalar.dma_start(xo_stage[32 * b : 32 * b + 4], by_pairs(xo_scales, b))
         nc.sync.dma_start(xt_tab[:].bitcast(I32), words(xt_words))
-        nc.sync.dma_start(lists[1][:], offs2)
         for i, src in enumerate((w_scales, w0_scales)):
             nc.sync.dma_start(ws_raw[0:4, :, i, :].bitcast(I32), src[0].bitcast(I32).rearrange("(q r) n -> r q n", r=4))
+        for b in range(2):
+            nc.sync.dma_start(xo_stage[64 + 32 * b : 64 + 32 * b + 4], by_pairs(xo_scales, b))
         nc.sync.dma_start(xo_tab[:].bitcast(I32), words(xo_words))
+        nc.sync.dma_start(lists[1][:], offs2)
+        nc.sync.dma_start(w_raw[0][:].bitcast(I32), w_words[0].bitcast(I32))
+        nc.sync.dma_start(w_raw[1][:].bitcast(I32), w0_words[0].bitcast(I32))
         nc.sync.dma_start(lists[2][:], offs3)
         nc.sync.dma_start(lists[3][:], offs4)
         nc.sync.dma_start(sa_t[:], sa.rearrange("(p t) o -> p (t o)", t=PACK))
@@ -106,21 +104,25 @@ def tile_list_ownreads_bank_one_plain_kernel(
             nc.vector.tensor_copy(got[:], tabs[i][0][:].indirect(tabs[i][2][:, 8 * half : 8 * half + 8]))
             return got
 
-        for i in range(2):
-            nc.scalar.copy(w_dealt[i][:], w_raw[i][:].rearrange("p (m t) -> p t m", t=PACK))
+        def deal_words(t0, t1):
+            for i in range(2):
+                nc.scalar.copy(w_dealt[i][:, t0:t1], w_raw[i][:].rearrange("p (m t) -> p t m", t=PACK)[:, t0:t1])
 
         def deal(t0, t1):
             nc.vector.tensor_copy(ws_dealt[:, t0:t1], ws_raw[:, 0].rearrange("p i (m t) -> p t i m", t=PACK)[:, t0:t1])
 
         got_s = [gather_scales(0, 0), None]
-        for a in range(2):
-            nc.vector.tensor_copy(xo_plane[64 * a : 64 * a + 64].bitcast(I32), xo_stage[:, a, :])
-        got_s[1] = gather_scales(1, 0)
         got_w = [gather_words(0, 0), None]
         for q in range(1, 4):
             nc.vector.tensor_copy(ws_raw[32 * q : 32 * q + 4, 0].bitcast(I32), ws_raw[0:4, q].bitcast(I32))
         deal(0, 1)
+        for a in range(2):
+            nc.vector.tensor_copy(xo_plane[64 * a : 64 * a + 64].bitcast(I32), xo_stage[64:128, a, :])
+        board.append(sb_tile([P, C], F32, "board2", tag="xo_stage"))
+        nc.gpsimd.memset(board[2][:], 0.0)
+        got_s[1] = gather_scales(1, 0)
         got_w[1] = gather_words(1, 0)
+        deal_words(0, 1)
 
         def product(acc, t):
             for i in range(2):
@@ -132,28 +134,33 @@ def tile_list_ownreads_bank_one_plain_kernel(
         def place(t, half, src):
             nc.scalar.activation(board[t][:].indirect(lists[2][:, 8 * half : 8 * half + 8]), src, COPY)
 
-        for t in range(PACK):
-            acc = psum.tile([P, HALF], F32, name="accA%d" % t)
-            product(acc[:], t)
-            a_sb = sb_tile([P, HALF], F32, "aA%d" % t)
-            if t == 0:
-                nc.scalar.activation(a_sb[:], acc[:], COPY)
-            else:
-                nc.vector.tensor_copy(a_sb[:], acc[:])
-            place(t, 0, a_sb[:])
-            if t == 0:
-                deal(1, PACK)
+        def sums(half, tiles, engine_copy):
+            acc = psum.tile([P, len(tiles), HALF], F32, name="acc%d_%d" % (half, tiles[0]))
+            for v, t in enumerate(tiles):
+                product(acc[:, v, :], t)
+            a_sb = sb_tile([P, len(tiles), HALF], F32, "a%d_%d" % (half, tiles[0]))
+            engine_copy(a_sb[:], acc[:])
+            return [a_sb[:, v, :] for v in range(len(tiles))]
+
+        def first_copy(dst, src):
+            deal_words(1, PACK)
+            nc.scalar.activation(dst, src, COPY)
+
+        place(0, 0, sums(0, [0], first_copy)[0])
+        deal(1, 2)
+        place(1, 0, sums(0, [1], nc.vector.tensor_copy)[0])
+        deal(2, PACK)
+        board.append(sb_tile([P, C], F32, "board3", tag="ws_raw"))
+        nc.gpsimd.memset(board[3][:], 0.0)
+        pair = sums(0, [2, 3], nc.vector.tensor_copy)
+        place(2, 0, pair[0])
+        place(3, 0, pair[1])
 
         got_s = [gather_scales(0, 1), gather_scales(1, 1)]
         got_w = [gather_words(0, 1), gather_words(1, 1)]
         a_second = []
-        for u in range(2):
-            acc = psum.tile([P, 2, HALF], F32, name="accB%d" % u)
-            for v in range(2):
-                product(acc[:, v, :], 2 * u + v)
-            a_sb = sb_tile([P, 2, HALF], F32, "aB%d" % u)
-            nc.vector.tensor_copy(a_sb[:], acc[:])
-            a_second.extend([a_sb[:, 0, :], a_sb[:, 1, :]])
+        for tiles in ([0], [1], [2, 3]):
+            a_second.extend(sums(1, tiles, nc.vector.tensor_copy))
 
         hid = sb_tile([P, O, PACK], BF16, "hid")
 

from contextlib import ExitStack

import concourse.mybir as mybir

FLOPS = 301989888

F32 = mybir.dt.float32
BF16 = mybir.dt.bfloat16
I32 = mybir.dt.int32
U32 = mybir.dt.uint32
U16 = mybir.dt.uint16
U8 = mybir.dt.uint8
E4M3 = mybir.dt.float8_e4m3fn_x4
E5M2 = mybir.dt.float8_e5m2_x4
E2M1 = mybir.dt.float4_e2m1fn_x4
COPY = mybir.ActivationFunctionType.Copy
MAX = mybir.AluOpType.max

P = 128
T = 1024
J = 256
R = 512
C = 512
O = 128
N = 256
PACK = 4
HALF = J // 2


def tile_list_ownreads_bank_one_plain_kernel(
    tc, xt_words, xt_scales, xo_words, xo_scales, w_words, w_scales, w0_words, w0_scales,
    sa, sb, wb_words, wb_scales, offs, offs2, offs3, offs4, offs5, out,
):
    nc = tc.nc
    with ExitStack() as ctx:
        keep = ctx.enter_context(tc.tile_pool(name="keep", bufs=1))
        psum = ctx.enter_context(tc.psum_pool(name="psum", bufs=1))

        def sb_tile(shape, dtype, name, tag=None):
            return keep.tile(shape, dtype, name=name, tag=tag or name, align_bytes=64)

        xt_stage = sb_tile([4, 4, T // 4], I32, "xt_stage")
        xo_stage = sb_tile([P, 2, T // 4], I32, "xo_stage")
        xt_plane = sb_tile([P, T], U8, "xt_plane")
        xo_plane = sb_tile([P, T], U8, "xo_plane")
        xt_tab = sb_tile([P, T], U32, "xt_tab")
        xo_tab = sb_tile([P, T], U32, "xo_tab")
        w_raw = [sb_tile([P, R], U16, "w_raw%d" % i) for i in range(2)]
        ws_raw = sb_tile([P, 4, 2, R], U8, "ws_raw")
        w_dealt = [sb_tile([P, PACK, P], U16, "w_dealt%d" % i) for i in range(2)]
        ws_dealt = sb_tile([P, PACK, 2, P], U8, "ws_dealt")
        lists = [sb_tile([P, 16], U16, "list%d" % i) for i in range(3)] + [sb_tile([P, 8], U16, "list%d" % i) for i in (3, 4)]
        sa_t = sb_tile([P, PACK], F32, "sa_t")
        sb_t = sb_tile([P, PACK], F32, "sb_t")
        wb_t = sb_tile([P, 2 * N], U8, "wb_t")
        wbs_t = sb_tile([P, N], U8, "wbs_t")
        board = [sb_tile([P, C], F32, "board%d" % t) for t in range(2)]

        nc.vector.memset(ws_raw[:, 0].bitcast(I32), 0)
        nc.vector.memset(xo_stage[64:128], 0)
        nc.vector.memset(xt_plane[:].bitcast(I32), 0)
        for t in range(2):
            nc.vector.memset(board[t][:], 0.0)
        nc.gpsimd.memset(wbs_t[:].bitcast(I32), 0)

        def words(ap):
            return ap[0].rearrange("p n t -> p (n t)").bitcast(I32)

        def by_pairs(ap, b):
            return ap[0].bitcast(I32).rearrange("(a b r) n -> b r a n", a=2, b=2)[b]

        nc.sync.dma_start(xt_stage[:], xt_scales[0].bitcast(I32).rearrange("(q r) n -> r q n", r=4))
        nc.sync.dma_start(lists[0][:], offs)
        nc.sync.dma_start(xt_tab[:].bitcast(I32), words(xt_words))
        for i, src in enumerate((w_scales, w0_scales)):
            nc.sync.dma_start(ws_raw[0:4, :, i, :].bitcast(I32), src[0].bitcast(I32).rearrange("(q r) n -> r q n", r=4))
        for b in range(2):
            nc.sync.dma_start(xo_stage[64 + 32 * b : 64 + 32 * b + 4], by_pairs(xo_scales, b))
        nc.sync.dma_start(xo_tab[:].bitcast(I32), words(xo_words))
        nc.sync.dma_start(lists[1][:], offs2)
        nc.sync.dma_start(w_raw[0][:].bitcast(I32), w_words[0].bitcast(I32))
        nc.sync.dma_start(w_raw[1][:].bitcast(I32), w0_words[0].bitcast(I32))
        nc.sync.dma_start(lists[2][:], offs3)
        nc.sync.dma_start(lists[3][:], offs4)
        nc.sync.dma_start(sa_t[:], sa.rearrange("(p t) o -> p (t o)", t=PACK))
        nc.sync.dma_start(lists[4][:], offs5)
        nc.sync.dma_start(sb_t[:], sb.rearrange("(p t) o -> p (t o)", t=PACK))
        nc.sync.dma_start(wb_t[:].bitcast(I32), wb_words[0].bitcast(I32))
        for q in range(4):
            nc.sync.dma_start(wbs_t[32 * q : 32 * q + 4].bitcast(I32), wb_scales[0, 4 * q : 4 * q + 4].bitcast(I32))

        for q in range(4):
            nc.vector.tensor_copy(xt_plane[32 * q : 32 * q + 4].bitcast(I32), xt_stage[:, q, :])

        tabs = ((xt_tab, xt_plane, lists[0], E5M2), (xo_tab, xo_plane, lists[1], E4M3))

        def gather_scales(i, half):
            got = sb_tile([P, HALF], U8, "got_s%d_%d" % (i, half), tag="got_s%d" % i)
            nc.vector.tensor_copy(got[:], tabs[i][1][:].indirect(tabs[i][2][:, 8 * half : 8 * half + 8]))
            return got

        def gather_words(i, half):
            got = sb_tile([P, HALF], U32, "got_w%d_%d" % (i, half), tag="got_w%d" % i)
            nc.vector.tensor_copy(got[:], tabs[i][0][:].indirect(tabs[i][2][:, 8 * half : 8 * half + 8]))
            return got

        def deal_words(t0, t1):
            for i in range(2):
                nc.scalar.copy(w_dealt[i][:, t0:t1], w_raw[i][:].rearrange("p (m t) -> p t m", t=PACK)[:, t0:t1])

        def deal(t0, t1):
            nc.vector.tensor_copy(ws_dealt[:, t0:t1], ws_raw[:, 0].rearrange("p i (m t) -> p t i m", t=PACK)[:, t0:t1])

        got_s = [gather_scales(0, 0), None]
        got_w = [gather_words(0, 0), None]
        for q in range(1, 4):
            nc.vector.tensor_copy(ws_raw[32 * q : 32 * q + 4, 0].bitcast(I32), ws_raw[0:4, q].bitcast(I32))
        deal(0, 1)
        for a in range(2):
            nc.vector.tensor_copy(xo_plane[64 * a : 64 * a + 64].bitcast(I32), xo_stage[64:128, a, :])
        board.append(sb_tile([P, C], F32, "board2", tag="xo_stage"))
        nc.gpsimd.memset(board[2][:], 0.0)
        got_s[1] = gather_scales(1, 0)
        got_w[1] = gather_words(1, 0)
        deal_words(0, 1)

        def product(acc, t):
            for i in range(2):
                nc.tensor.matmul_mx(
                    out=acc, lhsT=w_dealt[i][:, t, :].bitcast(E2M1), lhsT_scale=ws_dealt[:, t, i, :],
                    rhs=got_w[i][:].bitcast(tabs[i][3]), rhs_scale=got_s[i][:], start=(i == 0), stop=(i == 1),
                )

        def place(t, half, src):
            nc.scalar.activation(board[t][:].indirect(lists[2][:, 8 * half : 8 * half + 8]), src, COPY)

        def sums(half, tiles, engine_copy):
            acc = psum.tile([P, len(tiles), HALF], F32, name="acc%d_%d" % (half, tiles[0]))
            for v, t in enumerate(tiles):
                product(acc[:, v, :], t)
            a_sb = sb_tile([P, len(tiles), HALF], F32, "a%d_%d" % (half, tiles[0]))
            engine_copy(a_sb[:], acc[:])
            return [a_sb[:, v, :] for v in range(len(tiles))]

        def first_copy(dst, src):
            deal_words(1, PACK)
            nc.scalar.activation(dst, src, COPY)

        place(0, 0, sums(0, [0], first_copy)[0])
        deal(1, 2)
        place(1, 0, sums(0, [1], nc.vector.tensor_copy)[0])
        deal(2, PACK)
        board.append(sb_tile([P, C], F32, "board3", tag="ws_raw"))
        nc.gpsimd.memset(board[3][:], 0.0)
        pair = sums(0, [2, 3], nc.vector.tensor_copy)
        place(2, 0, pair[0])
        place(3, 0, pair[1])

        got_s = [gather_scales(0, 1), gather_scales(1, 1)]
        got_w = [gather_words(0, 1), gather_words(1, 1)]
        a_second = []
        for tiles in ([0], [1], [2, 3]):
            a_second.extend(sums(1, tiles, nc.vector.tensor_copy))

        hid = sb_tile([P, O, PACK], BF16, "hid")

        def fetch(t):
            ga = sb_tile([P, O], F32, "ga%d" % t)
            gb = sb_tile([P, O], F32, "gb%d" % t)
            nc.scalar.activation(ga[:], board[t][:].indirect(lists[3][:]), COPY, scale=sa_t[:, t : t + 1])
            nc.scalar.activation(gb[:], board[t][:].indirect(lists[4][:]), COPY, scale=sb_t[:, t : t + 1])
            nc.vector.tensor_tensor(hid[:, :, t], ga[:], gb[:], MAX)

        place(0, 1, a_second[0])
        for t in range(1, PACK):
            place(t, 1, a_second[t])
            fetch(t - 1)
        fetch(PACK - 1)

        codes = sb_tile([P, O], U32, "codes")
        plane = sb_tile([P, O], U8, "plane")
        nc.vector.quantize_mx(codes[:].bitcast(E4M3), plane[:], hid[:].rearrange("p o t -> p (o t)"))

        for h in range(2):
            acc = psum.tile([P, O], F32, name="accY%d" % h)
            nc.tensor.matmul_mx(
                out=acc[:], lhsT=wb_t[:, 2 * P * h : 2 * P * (h + 1)].bitcast(E2M1), lhsT_scale=wbs_t[:, P * h : P * (h + 1)],
                rhs=codes[:].bitcast(E4M3), rhs_scale=plane[:], start=True, stop=True,
            )
            y = sb_tile([P, O], F32, "y%d" % h)
            if h == 0:
                nc.vector.tensor_copy(y[:], acc[:])
                nc.sync.dma_start(out[0:P, :], y[:])
            else:
                nc.scalar.copy(y[:], acc[:])
                nc.scalar.dma_start(out[P : 2 * P, :], y[:])
